import numpy as np, ml_dtypes
CORES = [10,14,66,70,74,78,82,86,90,94,106,110]
N = 12
KB, QP = 4, 128
MEM = [6]
def setup_inputs(rng):
    q = rng.standard_normal((N, 128, QP), dtype=np.float32) / 4; k = rng.standard_normal((N, 128, KB * 128), dtype=np.float32)
    a = 2 * np.pi * rng.random((N, QP)); s = 400 * rng.random((N, QP)) ** 1.5; q[:, 0, :] = s * np.cos(a); q[:, 1, :] = s * np.sin(a); q[:, 2, :] = 150 * rng.standard_normal((N, QP)); k[:, 2, :] = 1 + k[:, 2, :] / 50
    c = np.zeros(N); c[MEM] = rng.permutation(len(MEM))
    a = (2 * np.pi * rng.random() + np.pi / 2 * (c.reshape(N, 1, 1) + 0.5) / len(MEM) - 0.5 + (np.arange(KB).reshape(1, KB, 1) + rng.random((N, KB, 128))) / KB).reshape(N, KB * 128); k[:, 0, :] = np.cos(a); k[:, 1, :] = np.sin(a)
    return {"q": q.astype(ml_dtypes.bfloat16), "k": k.astype(ml_dtypes.bfloat16), "v": rng.standard_normal((N, 128, KB * 128), dtype=np.float32).astype(ml_dtypes.bfloat16)}
def setup_inputs_big(rng):
    d = setup_inputs(rng)
    for k in ("v",): d[k] = (d[k].astype(np.float32) * 1048576.0).astype(d[k].dtype)
    return d
def setup_inputs_small(rng):
    d = setup_inputs(rng)
    for k in ("v",): d[k] = (d[k].astype(np.float32) * (1 / 1048576.0)).astype(d[k].dtype)
    return d
def reference(q, k, v):
    Q, K, V = q.astype(np.float64), k.astype(np.float64), v.astype(np.float64)
    y = np.zeros((N, QP, 128))
    for r in range(N):
        js = list(MEM)
        S = np.concatenate([K[j].T @ Q[r] for j in js], axis=0)
        P = np.exp(S - S.max(axis=0)); P = P / P.sum(axis=0)
        y[r] = P.T @ np.concatenate([V[j][:, 128 * b:128 * b + 128] for j in js for b in range(KB)], axis=0)
    return {"y": y.astype(ml_dtypes.bfloat16)}

@@ -1,0 +1,213 @@
+from concourse.bass import DstId, RemoteDMATransfer
+from concourse.mybir import AluOpType, AxisListType, ActivationFunctionType
+
+SIM_CORES = 112
+KB = 4
+MAXB = 8
+HEAD = 2
+NS, NP, NY = 3, 3, 2
+
+SCRATCH = {
+    "kbuf": ("sbuf", [128, 512], "bfloat16"),
+    "vbuf": ("sbuf", [128, 512], "bfloat16"),
+    "ones": ("sbuf", [128, 128], "bfloat16"),
+    "ident": ("sbuf", [128, 128], "bfloat16"),
+    "stat": ("sbuf", [128, 4 * MAXB], "float32"),
+    "qstage": ("dram", [128, 128], "bfloat16"),
+    "yland": ("dram", [128, 128], "bfloat16"),
+}
+for _i in range(MAXB):
+    SCRATCH["qin%d" % _i] = ("sbuf", [128, 128], "bfloat16")
+    SCRATCH["p%d" % _i] = ("sbuf", [128, 512], "bfloat16")
+    SCRATCH["pt%d" % _i] = ("sbuf", [128, 512], "bfloat16")
+    SCRATCH["ysb%d" % _i] = ("sbuf", [128, 128], "bfloat16")
+for _i in range(NS):
+    SCRATCH["S%d" % _i] = ("psum", [128, 512], "float32")
+for _i in range(NP):
+    SCRATCH["PT%d" % _i] = ("psum", [128, 1024], "bfloat16")
+for _i in range(NY):
+    SCRATCH["Y%d" % _i] = ("psum", [128, 512], "float32")
+
+SEMAPHORES = ["kar", "var", "one", "idn", "qld", "sent", "yarr", "done"]
+for _i in range(MAXB):
+    SEMAPHORES += [s + str(_i) for s in ("qa", "sS", "sM", "sE", "sT", "sC", "sR", "sV", "sY")]
+
+
+def _count(mask):
+    return bin(mask).count("1")
+
+
+def make_plan(T, topo):
+    cores = list(T.cores)
+    owner = cores[T.tables["MEM"][0]]
+    home = topo.chip(owner)
+    here = [c for c in range(SIM_CORES) if topo.chip(c) == home]
+    away = [c for c in cores if topo.chip(c) != home]
+    workers = [c for c in here if c == owner or c in cores or all(topo.may_write(c, r) for r in away)]
+    workers.sort(key=lambda c: (c != owner, c))
+    load = {c: 0.0 for c in workers}
+    for c in workers:
+        if c == owner:
+            load[c] = -float(HEAD)
+        elif c in cores:
+            load[c] = 0.5
+    work = {c: [] for c in workers}
+    for r in away:
+        ok = [c for c in workers if topo.may_write(c, r)]
+        h = min(ok, key=lambda c: load[c] + (0.25 if topo.die(c) != topo.die(r) else 0.0))
+        work[h].append(r)
+        load[h] += 1.0
+
+    def hops(r):
+        return 1 if (topo.mates(home, topo.chip(r)) or topo.same_plane(home, topo.chip(r))) else 2
+    for c in workers:
+        work[c].sort(key=hops)
+        if c == owner:
+            work[c].insert(0, c)
+        elif c in cores:
+            work[c].append(c)
+    return owner, work
+
+
+def _waiter(queue, T):
+    seen = {}
+
+    def w(name, val):
+        if seen.get(name, 0) < val:
+            seen[name] = val
+            queue.wait_ge(T.sem[name], val)
+    return w
+
+
+def client(g, core, T, topo, work):
+    h, slot = [(c, l.index(core)) for c, l in work.items() if core in l][0]
+    g.sync.dma_start(T.qstage[:, :], T.q[:, :]).then_inc(T.sem.qld, 16)
+    rid, pid, _ = topo.addr(h)
+    m = topo.mask(core, h)
+    g.wait_ge(T.sem.qld, 16)
+    g.remote_dma(T["qin%d" % slot][:, :], T.qstage[:, :], T.sem["qa%d" % slot], T.sem.sent, pid, rid, m)
+    g.sync.wait_ge(T.sem.yarr, _count(topo.mask(h, core)))
+    g.sync.dma_start(T.y[:, :], T.yland[:, :]).then_inc(T.sem.done, 16)
+    g.sync.wait_ge(T.sem.done, 16)
+    g.wait_ge(T.sem.sent, _count(m))
+
+
+def worker(g, core, T, topo, owner, work):
+    mine = work[core]
+    n = len(mine)
+    pe, dve, act, sp = g.tensor, g.vector, g.scalar, g.sync
+    wpe, wdve, wact, wg, wsp = _waiter(pe, T), _waiter(dve, T), _waiter(act, T), _waiter(g, T), _waiter(sp, T)
+    sent = [0]
+    others = [c for c in work if c != owner]
+    kvmask = topo.mask(owner, others[0])
+    for c in others:
+        kvmask &= topo.mask(owner, c)
+    kvn = 16 if core == owner else _count(kvmask)
+    qn = [16 if r == core else _count(topo.mask(r, core)) for r in mine]
+
+    if core == owner:
+        sp.dma_start(T.kbuf[:, :], T.k[:, :]).then_inc(T.sem.kar, 16)
+        act.dma_start(T["qin%d" % mine.index(core)][:, :], T.q[:, :]).then_inc(T.sem["qa%d" % mine.index(core)], 16)
+        act.dma_start(T.vbuf[:, :], T.v[:, :]).then_inc(T.sem.var, 16)
+    elif core in mine:
+        sp.dma_start(T["qin%d" % mine.index(core)][:, :], T.q[:, :]).then_inc(T.sem["qa%d" % mine.index(core)], 16)
+
+    dve.memset(T.ones[:, :], 1.0).then_inc(T.sem.one, 1)
+    wg("one", 1)
+    g.affine_select(T.ident[:, :], T.ones[:, :], [[-1, 128]], AluOpType.is_equal, 0.0, 0, 1).then_inc(T.sem.idn, 1)
+
+    if core == owner:
+        ids = []
+        for c in others:
+            rid, pid, _ = topo.addr(c)
+            ids.append(DstId(rid=rid, pnc=pid))
+        for name, sem in (("kbuf", "kar"), ("vbuf", "var")):
+            wg(sem, 16)
+            g.remote_dma_fused([RemoteDMATransfer(dst_ids=ids, dma_engine_mask=kvmask, remote_sem=T.sem[sem],
+                                                  srcs=[T[name][:, :]], dsts=[T[name][:, :] for _ in others],
+                                                  alu_op=0)], local_sem=T.sem.sent)
+            sent[0] += _count(kvmask)
+
+    def col(i, j):
+        return T.stat[:, 4 * i + j:4 * i + j + 1]
+
+    def blk(t, b):
+        return t[:, 128 * b:128 * b + 128]
+
+    def S(i):
+        s = T["S%d" % (i % NS)]
+        wpe("kar", kvn)
+        wpe("qa%d" % i, qn[i])
+        if i >= NS:
+            wpe("sE%d" % (i - NS), 1)
+        pe.matmul(s[:, :], T["qin%d" % i][:, :], T.kbuf[:, :], True, True).then_inc(T.sem["sS%d" % i], 1)
+        wdve("sS%d" % i, 1)
+        dve.tensor_reduce(col(i, 0), s[:, :], AxisListType.X, AluOpType.max, negate=True).then_inc(T.sem["sM%d" % i], 1)
+        wact("sM%d" % i, 1)
+        act.activation(T["p%d" % i][:, :], s[:, :], ActivationFunctionType.Exp, bias=col(i, 0), scale=1.0,
+                       accum_out=col(i, 1)).then_inc(T.sem["sE%d" % i], 1)
+
+    def TR(i):
+        t = T["PT%d" % (i % NP)]
+        wpe("idn", 1)
+        wpe("sE%d" % i, 1)
+        if i >= NP:
+            wpe("sC%d" % (i - NP), 1)
+        for b in range(KB):
+            pe.transpose(blk(t, b), blk(T["p%d" % i], b), T.ident[:, :]).then_inc(T.sem["sT%d" % i], 1)
+        wdve("sE%d" % i, 1)
+        dve.reciprocal(col(i, 2), col(i, 1)).then_inc(T.sem["sR%d" % i], 1)
+        wdve("sT%d" % i, KB)
+        dve.tensor_copy(T["pt%d" % i][:, :], t[:, 0:512]).then_inc(T.sem["sC%d" % i], 1)
+
+    def PV(i):
+        y = T["Y%d" % (i % NY)]
+        wpe("var", kvn)
+        wpe("sC%d" % i, 1)
+        if i >= NY:
+            wpe("sY%d" % (i - NY), 1)
+        for b in range(KB):
+            pe.matmul(y[:, 0:128], blk(T["pt%d" % i], b), blk(T.vbuf, b), b == 0, b == KB - 1).then_inc(T.sem["sV%d" % i], 1)
+        wdve("sV%d" % i, KB)
+        wdve("sR%d" % i, 1)
+        dve.tensor_scalar(T["ysb%d" % i][:, :], y[:, 0:128], col(i, 2), None, AluOpType.mult).then_inc(T.sem["sY%d" % i], 1)
+        r = mine[i]
+        if r == core:
+            wsp("sY%d" % i, 1)
+            sp.dma_start(T.y[:, :], T["ysb%d" % i][:, :]).then_inc(T.sem.done, 16)
+            wsp("done", 16)
+        else:
+            rid, pid, _ = topo.addr(r)
+            m = topo.mask(core, r)
+            wg("sY%d" % i, 1)
+            g.remote_dma(T.yland[:, :], T["ysb%d" % i][:, :], T.sem.yarr, T.sem.sent, pid, rid, m)
+            sent[0] += _count(m)
+
+    def pipeline(L):
+        m = len(L)
+        for j in range(min(3, m)):
+            S(L[j])
+        for j in range(m):
+            TR(L[j])
+            if j >= 1:
+                PV(L[j - 1])
+            if j + 3 < m:
+                S(L[j + 3])
+        if m:
+            PV(L[m - 1])
+
+    if core == owner:
+        pipeline([0])
+        pipeline(list(range(1, n)))
+    else:
+        pipeline(list(range(n)))
+    if sent[0]:
+        g.wait_ge(T.sem.sent, sent[0])
+
+
+def rank_program(g, core, T, topo):
+    owner, work = make_plan(T, topo)
+    if core in work:
+        worker(g, core, T, topo, owner, work)
+    elif T.rank_of(core) is not None:
+        client(g, core, T, topo, work)

@@ -3,16 +3,18 @@ from concourse.mybir import AluOpType, AxisListType, ActivationFunctionType
 
 SIM_CORES = 112
 KB = 4
-MAXB = 8
-HEAD = 2
-NS, NP, NY = 3, 3, 2
+MAXB = 5
+HEAD = 0
+EXTRA = 1
+NS, NP, NY = 3, 4, 1
 
 SCRATCH = {
     "kbuf": ("sbuf", [128, 512], "bfloat16"),
     "vbuf": ("sbuf", [128, 512], "bfloat16"),
     "ones": ("sbuf", [128, 128], "bfloat16"),
     "ident": ("sbuf", [128, 128], "bfloat16"),
-    "stat": ("sbuf", [128, 4 * MAXB], "float32"),
+    "stat": ("sbuf", [128, 8 * MAXB], "float32"),
+    "run": ("sbuf", [128, 8], "float32"),
     "qstage": ("dram", [128, 128], "bfloat16"),
     "yland": ("dram", [128, 128], "bfloat16"),
 }
@@ -28,9 +30,10 @@ for _i in range(NP):
 for _i in range(NY):
     SCRATCH["Y%d" % _i] = ("psum", [128, 512], "float32")
 
-SEMAPHORES = ["kar", "var", "one", "idn", "qld", "sent", "yarr", "done"]
+SEMAPHORES = ["kar", "var", "one", "idn", "qld", "sent", "yarr", "done", "sA", "sMa", "sMr", "sEa", "sW", "sL"]
 for _i in range(MAXB):
-    SEMAPHORES += [s + str(_i) for s in ("qa", "sS", "sM", "sE", "sT", "sC", "sR", "sV", "sY")]
+    SEMAPHORES += [s + str(_i) for s in ("qa", "sS", "sM", "sN", "sR", "sV", "sY")]
+    SEMAPHORES += ["%s%d_%d" % (s, _i, b) for s in ("sE", "sT", "sC") for b in range(KB)]
 
 
 def _count(mask):
@@ -43,30 +46,30 @@ def make_plan(T, topo):
     home = topo.chip(owner)
     here = [c for c in range(SIM_CORES) if topo.chip(c) == home]
     away = [c for c in cores if topo.chip(c) != home]
-    workers = [c for c in here if c == owner or c in cores or all(topo.may_write(c, r) for r in away)]
-    workers.sort(key=lambda c: (c != owner, c))
-    load = {c: 0.0 for c in workers}
-    for c in workers:
-        if c == owner:
-            load[c] = -float(HEAD)
-        elif c in cores:
+    here.sort(key=lambda c: (c != owner, c))
+    team = [c for c in here if c in cores or all(topo.may_write(c, r) for r in away)]
+    team += [c for c in here if c not in team and topo.die(c) == topo.die(owner)][:EXTRA]
+    load = {c: 0.0 for c in team}
+    load[owner] = -float(HEAD)
+    for c in team:
+        if c != owner and c in cores:
             load[c] = 0.5
-    work = {c: [] for c in workers}
-    for r in away:
-        ok = [c for c in workers if topo.may_write(c, r)]
-        h = min(ok, key=lambda c: load[c] + (0.25 if topo.die(c) != topo.die(r) else 0.0))
+    work = {c: [] for c in team}
+    allowed = {r: [c for c in team if topo.may_write(c, r)] for r in away}
+    for r in sorted(away, key=lambda r: len(allowed[r])):
+        h = min(allowed[r], key=lambda c: load[c] + (0.25 if topo.die(c) != topo.die(r) else 0.0))
         work[h].append(r)
         load[h] += 1.0
 
     def hops(r):
         return 1 if (topo.mates(home, topo.chip(r)) or topo.same_plane(home, topo.chip(r))) else 2
-    for c in workers:
+    for c in team:
         work[c].sort(key=hops)
         if c == owner:
             work[c].insert(0, c)
         elif c in cores:
             work[c].append(c)
-    return owner, work
+    return owner, {c: l for c, l in work.items() if l}
 
 
 def _waiter(queue, T):
@@ -102,8 +105,16 @@ def worker(g, core, T, topo, owner, work):
     kvmask = topo.mask(owner, others[0])
     for c in others:
         kvmask &= topo.mask(owner, c)
-    kvn = 16 if core == owner else _count(kvmask)
+    bits = [1 << e for e in range(16) if kvmask >> e & 1]
+    near = [c for c in others if topo.die(c) == topo.die(owner)]
+    far = [c for c in others if topo.die(c) != topo.die(owner)]
+    if near and far:
+        parts = [(far, sum(bits[0::2])), (near, sum(bits[1::2]))]
+    else:
+        parts = [(others, kvmask)]
+    kvn = 16 if core == owner else [_count(m) for l, m in parts if core in l][0]
     qn = [16 if r == core else _count(topo.mask(r, core)) for r in mine]
+    Exp = ActivationFunctionType.Exp
 
     if core == owner:
         sp.dma_start(T.kbuf[:, :], T.k[:, :]).then_inc(T.sem.kar, 16)
@@ -117,60 +128,99 @@ def worker(g, core, T, topo, owner, work):
     g.affine_select(T.ident[:, :], T.ones[:, :], [[-1, 128]], AluOpType.is_equal, 0.0, 0, 1).then_inc(T.sem.idn, 1)
 
     if core == owner:
-        ids = []
-        for c in others:
-            rid, pid, _ = topo.addr(c)
-            ids.append(DstId(rid=rid, pnc=pid))
         for name, sem in (("kbuf", "kar"), ("vbuf", "var")):
+            trs = []
+            for dsts, m in parts:
+                ids = []
+                for c in dsts:
+                    rid, pid, _ = topo.addr(c)
+                    ids.append(DstId(rid=rid, pnc=pid))
+                trs.append(RemoteDMATransfer(dst_ids=ids, dma_engine_mask=m, remote_sem=T.sem[sem],
+                                             srcs=[T[name][:, :]], dsts=[T[name][:, :] for _ in dsts], alu_op=0))
+                sent[0] += _count(m)
             wg(sem, 16)
-            g.remote_dma_fused([RemoteDMATransfer(dst_ids=ids, dma_engine_mask=kvmask, remote_sem=T.sem[sem],
-                                                  srcs=[T[name][:, :]], dsts=[T[name][:, :] for _ in others],
-                                                  alu_op=0)], local_sem=T.sem.sent)
-            sent[0] += _count(kvmask)
+            g.remote_dma_fused(trs, local_sem=T.sem.sent)
 
     def col(i, j):
-        return T.stat[:, 4 * i + j:4 * i + j + 1]
+        return T.stat[:, 8 * i + j:8 * i + j + 1]
+
+    def rc(j):
+        return T.run[:, j:j + 1]
 
     def blk(t, b):
         return t[:, 128 * b:128 * b + 128]
 
+    split = set() if core == owner else {0}
+    sa = T.Y0[:, 128:256]
+
     def S(i):
         s = T["S%d" % (i % NS)]
+        q = T["qin%d" % i][:, :]
+        p = T["p%d" % i]
+        first = 0
         wpe("kar", kvn)
         wpe("qa%d" % i, qn[i])
-        if i >= NS:
-            wpe("sE%d" % (i - NS), 1)
-        pe.matmul(s[:, :], T["qin%d" % i][:, :], T.kbuf[:, :], True, True).then_inc(T.sem["sS%d" % i], 1)
-        wdve("sS%d" % i, 1)
-        dve.tensor_reduce(col(i, 0), s[:, :], AxisListType.X, AluOpType.max, negate=True).then_inc(T.sem["sM%d" % i], 1)
-        wact("sM%d" % i, 1)
-        act.activation(T["p%d" % i][:, :], s[:, :], ActivationFunctionType.Exp, bias=col(i, 0), scale=1.0,
-                       accum_out=col(i, 1)).then_inc(T.sem["sE%d" % i], 1)
+        if i in split:
+            first = 1
+            pe.matmul(sa, q, T.kbuf[:, 0:128], True, True).then_inc(T.sem.sA, 1)
+            pe.matmul(s[:, 128:512], q, T.kbuf[:, 128:512], True, True).then_inc(T.sem["sS%d" % i], 1)
+            wdve("sA", 1)
+            dve.tensor_reduce(rc(0), sa, AxisListType.X, AluOpType.max, negate=True).then_inc(T.sem.sMa, 1)
+            wdve("sS%d" % i, 1)
+            dve.tensor_reduce(rc(1), s[:, 128:512], AxisListType.X, AluOpType.max, negate=True).then_inc(T.sem.sMr, 1)
+            wdve("sMa", 1)
+            wdve("sMr", 1)
+            dve.tensor_tensor(col(i, 0), rc(0), rc(1), AluOpType.min).then_inc(T.sem["sM%d" % i], 1)
+            wact("sMa", 1)
+            act.activation(p[:, 0:128], sa, Exp, bias=rc(0), scale=1.0, accum_out=col(i, 4)).then_inc(T.sem.sEa, 1)
+            wact("sM%d" % i, 1)
+            act.activation(rc(4), rc(0), Exp, bias=col(i, 0), scale=-1.0).then_inc(T.sem.sW, 1)
+        else:
+            if i >= NS:
+                for b in range(KB):
+                    wpe("sE%d_%d" % (i - NS, b), 1)
+            pe.matmul(s[:, :], q, T.kbuf[:, :], True, True).then_inc(T.sem["sS%d" % i], 1)
+            wdve("sS%d" % i, 1)
+            dve.tensor_reduce(col(i, 0), s[:, :], AxisListType.X, AluOpType.max,
+                              negate=True).then_inc(T.sem["sM%d" % i], 1)
+            wact("sM%d" % i, 1)
+        for b in range(first, KB):
+            act.activation(blk(p, b), blk(s, b), Exp, bias=col(i, 0), scale=1.0,
+                           accum_out=col(i, 4 + b)).then_inc(T.sem["sE%d_%d" % (i, b)], 1)
 
-    def TR(i):
-        t = T["PT%d" % (i % NP)]
+    def TRPV(i):
+        p = T["p%d" % i]
+        y = T.Y0[:, 0:128]
+        if i in split:
+            wdve("sW", 1)
+            wdve("sEa", 1)
+            dve.tensor_scalar(p[:, 0:128], p[:, 0:128], rc(4), None, AluOpType.mult).then_inc(T.sem["sE%d_0" % i], 1)
+            dve.tensor_scalar(col(i, 4), col(i, 4), rc(4), None, AluOpType.mult).then_inc(T.sem.sL, 1)
         wpe("idn", 1)
-        wpe("sE%d" % i, 1)
-        if i >= NP:
-            wpe("sC%d" % (i - NP), 1)
         for b in range(KB):
-            pe.transpose(blk(t, b), blk(T["p%d" % i], b), T.ident[:, :]).then_inc(T.sem["sT%d" % i], 1)
-        wdve("sE%d" % i, 1)
+            wpe("sE%d_%d" % (i, b), 1)
+            if i >= 1:
+                wpe("sC%d_%d" % (i - 1, b), 1)
+            pe.transpose(T["PT%d" % b][:, 0:128], blk(p, b), T.ident[:, :]).then_inc(T.sem["sT%d_%d" % (i, b)], 1)
+            wdve("sT%d_%d" % (i, b), 1)
+            dve.tensor_copy(blk(T["pt%d" % i], b), T["PT%d" % b][:, 0:128]).then_inc(T.sem["sC%d_%d" % (i, b)], 1)
+        for b in range(KB):
+            wdve("sE%d_%d" % (i, b), 1)
+        if i in split:
+            wdve("sL", 1)
+        dve.tensor_reduce(col(i, 1), T.stat[:, 8 * i + 4:8 * i + 8], AxisListType.X,
+                          AluOpType.add).then_inc(T.sem["sN%d" % i], 1)
+        wdve("sN%d" % i, 1)
         dve.reciprocal(col(i, 2), col(i, 1)).then_inc(T.sem["sR%d" % i], 1)
-        wdve("sT%d" % i, KB)
-        dve.tensor_copy(T["pt%d" % i][:, :], t[:, 0:512]).then_inc(T.sem["sC%d" % i], 1)
-
-    def PV(i):
-        y = T["Y%d" % (i % NY)]
         wpe("var", kvn)
-        wpe("sC%d" % i, 1)
-        if i >= NY:
-            wpe("sY%d" % (i - NY), 1)
+        if i >= 1:
+            wpe("sY%d" % (i - 1), 1)
         for b in range(KB):
-            pe.matmul(y[:, 0:128], blk(T["pt%d" % i], b), blk(T.vbuf, b), b == 0, b == KB - 1).then_inc(T.sem["sV%d" % i], 1)
+            wpe("sC%d_%d" % (i, b), 1)
+            pe.matmul(y, blk(T["pt%d" % i], b), blk(T.vbuf, b), b == 0, b == KB - 1).then_inc(T.sem["sV%d" % i], 1)
         wdve("sV%d" % i, KB)
         wdve("sR%d" % i, 1)
-        dve.tensor_scalar(T["ysb%d" % i][:, :], y[:, 0:128], col(i, 2), None, AluOpType.mult).then_inc(T.sem["sY%d" % i], 1)
+        dve.tensor_scalar(T["ysb%d" % i][:, :], y, col(i, 2), None, AluOpType.mult).then_inc(T.sem["sY%d" % i], 1)
         r = mine[i]
         if r == core:
             wsp("sY%d" % i, 1)
@@ -185,16 +235,12 @@ def worker(g, core, T, topo, owner, work):
 
     def pipeline(L):
         m = len(L)
-        for j in range(min(3, m)):
+        for j in range(min(NS, m)):
             S(L[j])
         for j in range(m):
-            TR(L[j])
-            if j >= 1:
-                PV(L[j - 1])
-            if j + 3 < m:
-                S(L[j + 3])
-        if m:
-            PV(L[m - 1])
+            TRPV(L[j])
+            if j + NS < m:
+                S(L[j + NS])
 
     if core == owner:
         pipeline([0])

@@ -11,7 +11,7 @@ NS, NP, NY = 3, 4, 1
 SCRATCH = {
     "kbuf": ("sbuf", [128, 512], "bfloat16"),
     "vbuf": ("sbuf", [128, 512], "bfloat16"),
-    "ones": ("sbuf", [128, 128], "bfloat16"),
+    "mask": ("sbuf", [128, 128], "bfloat16"),
     "ident": ("sbuf", [128, 128], "bfloat16"),
     "stat": ("sbuf", [128, 8 * MAXB], "float32"),
     "run": ("sbuf", [128, 8], "float32"),
@@ -30,7 +30,7 @@ for _i in range(NP):
 for _i in range(NY):
     SCRATCH["Y%d" % _i] = ("psum", [128, 512], "float32")
 
-SEMAPHORES = ["kar", "var", "one", "idn", "qld", "sent", "yarr", "done", "sA", "sMa", "sMr", "sEa", "sW", "sL"]
+SEMAPHORES = ["kar", "var", "one", "msk", "idn", "qld", "sent", "yarr", "done", "sA", "sMa", "sMr"]
 for _i in range(MAXB):
     SEMAPHORES += [s + str(_i) for s in ("qa", "sS", "sM", "sN", "sR", "sV", "sY")]
     SEMAPHORES += ["%s%d_%d" % (s, _i, b) for s in ("sE", "sT", "sC") for b in range(KB)]
@@ -123,9 +123,11 @@ def worker(g, core, T, topo, owner, work):
     elif core in mine:
         sp.dma_start(T["qin%d" % mine.index(core)][:, :], T.q[:, :]).then_inc(T.sem["qa%d" % mine.index(core)], 16)
 
-    dve.memset(T.ones[:, :], 1.0).then_inc(T.sem.one, 1)
+    dve.memset(T.mask[:, :], 0.0).then_inc(T.sem.one, 1)
     wg("one", 1)
-    g.affine_select(T.ident[:, :], T.ones[:, :], [[-1, 128]], AluOpType.is_equal, 0.0, 0, 1).then_inc(T.sem.idn, 1)
+    g.affine_select(T.mask[:, :], T.mask[:, :], [[-1, 128]], AluOpType.is_equal, -200.0, 0, 1).then_inc(T.sem.msk, 1)
+    wact("msk", 1)
+    act.activation(T.ident[:, :], T.mask[:, :], Exp).then_inc(T.sem.idn, 1)
 
     if core == owner:
         for name, sem in (("kbuf", "kar"), ("vbuf", "var")):
@@ -150,31 +152,26 @@ def worker(g, core, T, topo, owner, work):
     def blk(t, b):
         return t[:, 128 * b:128 * b + 128]
 
-    split = set() if core == owner else {0}
-    sa = T.Y0[:, 128:256]
+    split = {0}
+    sa = T.Y0[:, 256:512]
 
     def S(i):
         s = T["S%d" % (i % NS)]
         q = T["qin%d" % i][:, :]
         p = T["p%d" % i]
-        first = 0
         wpe("kar", kvn)
         wpe("qa%d" % i, qn[i])
         if i in split:
-            first = 1
-            pe.matmul(sa, q, T.kbuf[:, 0:128], True, True).then_inc(T.sem.sA, 1)
-            pe.matmul(s[:, 128:512], q, T.kbuf[:, 128:512], True, True).then_inc(T.sem["sS%d" % i], 1)
+            pe.matmul(sa, q, T.kbuf[:, 0:256], True, True).then_inc(T.sem.sA, 1)
+            pe.matmul(s[:, 256:512], q, T.kbuf[:, 256:512], True, True).then_inc(T.sem["sS%d" % i], 1)
             wdve("sA", 1)
             dve.tensor_reduce(rc(0), sa, AxisListType.X, AluOpType.max, negate=True).then_inc(T.sem.sMa, 1)
             wdve("sS%d" % i, 1)
-            dve.tensor_reduce(rc(1), s[:, 128:512], AxisListType.X, AluOpType.max, negate=True).then_inc(T.sem.sMr, 1)
+            dve.tensor_reduce(rc(1), s[:, 256:512], AxisListType.X, AluOpType.max, negate=True).then_inc(T.sem.sMr, 1)
             wdve("sMa", 1)
             wdve("sMr", 1)
             dve.tensor_tensor(col(i, 0), rc(0), rc(1), AluOpType.min).then_inc(T.sem["sM%d" % i], 1)
-            wact("sMa", 1)
-            act.activation(p[:, 0:128], sa, Exp, bias=rc(0), scale=1.0, accum_out=col(i, 4)).then_inc(T.sem.sEa, 1)
             wact("sM%d" % i, 1)
-            act.activation(rc(4), rc(0), Exp, bias=col(i, 0), scale=-1.0).then_inc(T.sem.sW, 1)
         else:
             if i >= NS:
                 for b in range(KB):
@@ -184,18 +181,14 @@ def worker(g, core, T, topo, owner, work):
             dve.tensor_reduce(col(i, 0), s[:, :], AxisListType.X, AluOpType.max,
                               negate=True).then_inc(T.sem["sM%d" % i], 1)
             wact("sM%d" % i, 1)
-        for b in range(first, KB):
-            act.activation(blk(p, b), blk(s, b), Exp, bias=col(i, 0), scale=1.0,
+        for b in range(KB):
+            src = blk(T.Y0, b + 2) if (i in split and b < 2) else blk(s, b)
+            act.activation(blk(p, b), src, Exp, bias=col(i, 0), scale=1.0,
                            accum_out=col(i, 4 + b)).then_inc(T.sem["sE%d_%d" % (i, b)], 1)
 
     def TRPV(i):
         p = T["p%d" % i]
         y = T.Y0[:, 0:128]
-        if i in split:
-            wdve("sW", 1)
-            wdve("sEa", 1)
-            dve.tensor_scalar(p[:, 0:128], p[:, 0:128], rc(4), None, AluOpType.mult).then_inc(T.sem["sE%d_0" % i], 1)
-            dve.tensor_scalar(col(i, 4), col(i, 4), rc(4), None, AluOpType.mult).then_inc(T.sem.sL, 1)
         wpe("idn", 1)
         for b in range(KB):
             wpe("sE%d_%d" % (i, b), 1)
@@ -206,8 +199,6 @@ def worker(g, core, T, topo, owner, work):
             dve.tensor_copy(blk(T["pt%d" % i], b), T["PT%d" % b][:, 0:128]).then_inc(T.sem["sC%d_%d" % (i, b)], 1)
         for b in range(KB):
             wdve("sE%d_%d" % (i, b), 1)
-        if i in split:
-            wdve("sL", 1)
         dve.tensor_reduce(col(i, 1), T.stat[:, 8 * i + 4:8 * i + 8], AxisListType.X,
                           AluOpType.add).then_inc(T.sem["sN%d" % i], 1)
         wdve("sN%d" % i, 1)

from concourse.bass import DstId, RemoteDMATransfer
from concourse.mybir import AluOpType, AxisListType, ActivationFunctionType

SIM_CORES = 112
KB = 4
MAXB = 5
HEAD = 0
EXTRA = 1
NS, NP, NY = 3, 4, 1

SCRATCH = {
    "kbuf": ("sbuf", [128, 512], "bfloat16"),
    "vbuf": ("sbuf", [128, 512], "bfloat16"),
    "mask": ("sbuf", [128, 128], "bfloat16"),
    "ident": ("sbuf", [128, 128], "bfloat16"),
    "stat": ("sbuf", [128, 8 * MAXB], "float32"),
    "run": ("sbuf", [128, 8], "float32"),
    "qstage": ("dram", [128, 128], "bfloat16"),
    "yland": ("dram", [128, 128], "bfloat16"),
}
for _i in range(MAXB):
    SCRATCH["qin%d" % _i] = ("sbuf", [128, 128], "bfloat16")
    SCRATCH["p%d" % _i] = ("sbuf", [128, 512], "bfloat16")
    SCRATCH["pt%d" % _i] = ("sbuf", [128, 512], "bfloat16")
    SCRATCH["ysb%d" % _i] = ("sbuf", [128, 128], "bfloat16")
for _i in range(NS):
    SCRATCH["S%d" % _i] = ("psum", [128, 512], "float32")
for _i in range(NP):
    SCRATCH["PT%d" % _i] = ("psum", [128, 1024], "bfloat16")
for _i in range(NY):
    SCRATCH["Y%d" % _i] = ("psum", [128, 512], "float32")

SEMAPHORES = ["kar", "var", "one", "msk", "idn", "qld", "sent", "yarr", "done", "sA", "sMa", "sMr"]
for _i in range(MAXB):
    SEMAPHORES += [s + str(_i) for s in ("qa", "sS", "sM", "sN", "sR", "sV", "sY")]
    SEMAPHORES += ["%s%d_%d" % (s, _i, b) for s in ("sE", "sT", "sC") for b in range(KB)]


def _count(mask):
    return bin(mask).count("1")


def make_plan(T, topo):
    cores = list(T.cores)
    owner = cores[T.tables["MEM"][0]]
    home = topo.chip(owner)
    here = [c for c in range(SIM_CORES) if topo.chip(c) == home]
    away = [c for c in cores if topo.chip(c) != home]
    here.sort(key=lambda c: (c != owner, c))
    team = [c for c in here if c in cores or all(topo.may_write(c, r) for r in away)]
    team += [c for c in here if c not in team and topo.die(c) == topo.die(owner)][:EXTRA]
    load = {c: 0.0 for c in team}
    load[owner] = -float(HEAD)
    for c in team:
        if c != owner and c in cores:
            load[c] = 0.5
    work = {c: [] for c in team}
    allowed = {r: [c for c in team if topo.may_write(c, r)] for r in away}
    for r in sorted(away, key=lambda r: len(allowed[r])):
        h = min(allowed[r], key=lambda c: load[c] + (0.25 if topo.die(c) != topo.die(r) else 0.0))
        work[h].append(r)
        load[h] += 1.0

    def hops(r):
        return 1 if (topo.mates(home, topo.chip(r)) or topo.same_plane(home, topo.chip(r))) else 2
    for c in team:
        work[c].sort(key=hops)
        if c == owner:
            work[c].insert(0, c)
        elif c in cores:
            work[c].append(c)
    return owner, {c: l for c, l in work.items() if l}


def _waiter(queue, T):
    seen = {}

    def w(name, val):
        if seen.get(name, 0) < val:
            seen[name] = val
            queue.wait_ge(T.sem[name], val)
    return w


def client(g, core, T, topo, work):
    h, slot = [(c, l.index(core)) for c, l in work.items() if core in l][0]
    g.sync.dma_start(T.qstage[:, :], T.q[:, :]).then_inc(T.sem.qld, 16)
    rid, pid, _ = topo.addr(h)
    m = topo.mask(core, h)
    g.wait_ge(T.sem.qld, 16)
    g.remote_dma(T["qin%d" % slot][:, :], T.qstage[:, :], T.sem["qa%d" % slot], T.sem.sent, pid, rid, m)
    g.sync.wait_ge(T.sem.yarr, _count(topo.mask(h, core)))
    g.sync.dma_start(T.y[:, :], T.yland[:, :]).then_inc(T.sem.done, 16)
    g.sync.wait_ge(T.sem.done, 16)
    g.wait_ge(T.sem.sent, _count(m))


def worker(g, core, T, topo, owner, work):
    mine = work[core]
    n = len(mine)
    pe, dve, act, sp = g.tensor, g.vector, g.scalar, g.sync
    wpe, wdve, wact, wg, wsp = _waiter(pe, T), _waiter(dve, T), _waiter(act, T), _waiter(g, T), _waiter(sp, T)
    sent = [0]
    others = [c for c in work if c != owner]
    kvmask = topo.mask(owner, others[0])
    for c in others:
        kvmask &= topo.mask(owner, c)
    bits = [1 << e for e in range(16) if kvmask >> e & 1]
    near = [c for c in others if topo.die(c) == topo.die(owner)]
    far = [c for c in others if topo.die(c) != topo.die(owner)]
    if near and far:
        parts = [(far, sum(bits[0::2])), (near, sum(bits[1::2]))]
    else:
        parts = [(others, kvmask)]
    kvn = 16 if core == owner else [_count(m) for l, m in parts if core in l][0]
    qn = [16 if r == core else _count(topo.mask(r, core)) for r in mine]
    Exp = ActivationFunctionType.Exp

    if core == owner:
        sp.dma_start(T.kbuf[:, :], T.k[:, :]).then_inc(T.sem.kar, 16)
        act.dma_start(T["qin%d" % mine.index(core)][:, :], T.q[:, :]).then_inc(T.sem["qa%d" % mine.index(core)], 16)
        act.dma_start(T.vbuf[:, :], T.v[:, :]).then_inc(T.sem.var, 16)
    elif core in mine:
        sp.dma_start(T["qin%d" % mine.index(core)][:, :], T.q[:, :]).then_inc(T.sem["qa%d" % mine.index(core)], 16)

    dve.memset(T.mask[:, :], 0.0).then_inc(T.sem.one, 1)
    wg("one", 1)
    g.affine_select(T.mask[:, :], T.mask[:, :], [[-1, 128]], AluOpType.is_equal, -200.0, 0, 1).then_inc(T.sem.msk, 1)
    wact("msk", 1)
    act.activation(T.ident[:, :], T.mask[:, :], Exp).then_inc(T.sem.idn, 1)

    if core == owner:
        for name, sem in (("kbuf", "kar"), ("vbuf", "var")):
            trs = []
            for dsts, m in parts:
                ids = []
                for c in dsts:
                    rid, pid, _ = topo.addr(c)
                    ids.append(DstId(rid=rid, pnc=pid))
                trs.append(RemoteDMATransfer(dst_ids=ids, dma_engine_mask=m, remote_sem=T.sem[sem],
                                             srcs=[T[name][:, :]], dsts=[T[name][:, :] for _ in dsts], alu_op=0))
                sent[0] += _count(m)
            wg(sem, 16)
            g.remote_dma_fused(trs, local_sem=T.sem.sent)

    def col(i, j):
        return T.stat[:, 8 * i + j:8 * i + j + 1]

    def rc(j):
        return T.run[:, j:j + 1]

    def blk(t, b):
        return t[:, 128 * b:128 * b + 128]

    split = {0}
    sa = T.Y0[:, 256:512]

    def S(i):
        s = T["S%d" % (i % NS)]
        q = T["qin%d" % i][:, :]
        p = T["p%d" % i]
        wpe("kar", kvn)
        wpe("qa%d" % i, qn[i])
        if i in split:
            pe.matmul(sa, q, T.kbuf[:, 0:256], True, True).then_inc(T.sem.sA, 1)
            pe.matmul(s[:, 256:512], q, T.kbuf[:, 256:512], True, True).then_inc(T.sem["sS%d" % i], 1)
            wdve("sA", 1)
            dve.tensor_reduce(rc(0), sa, AxisListType.X, AluOpType.max, negate=True).then_inc(T.sem.sMa, 1)
            wdve("sS%d" % i, 1)
            dve.tensor_reduce(rc(1), s[:, 256:512], AxisListType.X, AluOpType.max, negate=True).then_inc(T.sem.sMr, 1)
            wdve("sMa", 1)
            wdve("sMr", 1)
            dve.tensor_tensor(col(i, 0), rc(0), rc(1), AluOpType.min).then_inc(T.sem["sM%d" % i], 1)
            wact("sM%d" % i, 1)
        else:
            if i >= NS:
                for b in range(KB):
                    wpe("sE%d_%d" % (i - NS, b), 1)
            pe.matmul(s[:, :], q, T.kbuf[:, :], True, True).then_inc(T.sem["sS%d" % i], 1)
            wdve("sS%d" % i, 1)
            dve.tensor_reduce(col(i, 0), s[:, :], AxisListType.X, AluOpType.max,
                              negate=True).then_inc(T.sem["sM%d" % i], 1)
            wact("sM%d" % i, 1)
        for b in range(KB):
            src = blk(T.Y0, b + 2) if (i in split and b < 2) else blk(s, b)
            act.activation(blk(p, b), src, Exp, bias=col(i, 0), scale=1.0,
                           accum_out=col(i, 4 + b)).then_inc(T.sem["sE%d_%d" % (i, b)], 1)

    def TRPV(i):
        p = T["p%d" % i]
        y = T.Y0[:, 0:128]
        wpe("idn", 1)
        for b in range(KB):
            wpe("sE%d_%d" % (i, b), 1)
            if i >= 1:
                wpe("sC%d_%d" % (i - 1, b), 1)
            pe.transpose(T["PT%d" % b][:, 0:128], blk(p, b), T.ident[:, :]).then_inc(T.sem["sT%d_%d" % (i, b)], 1)
            wdve("sT%d_%d" % (i, b), 1)
            dve.tensor_copy(blk(T["pt%d" % i], b), T["PT%d" % b][:, 0:128]).then_inc(T.sem["sC%d_%d" % (i, b)], 1)
        for b in range(KB):
            wdve("sE%d_%d" % (i, b), 1)
        dve.tensor_reduce(col(i, 1), T.stat[:, 8 * i + 4:8 * i + 8], AxisListType.X,
                          AluOpType.add).then_inc(T.sem["sN%d" % i], 1)
        wdve("sN%d" % i, 1)
        dve.reciprocal(col(i, 2), col(i, 1)).then_inc(T.sem["sR%d" % i], 1)
        wpe("var", kvn)
        if i >= 1:
            wpe("sY%d" % (i - 1), 1)
        for b in range(KB):
            wpe("sC%d_%d" % (i, b), 1)
            pe.matmul(y, blk(T["pt%d" % i], b), blk(T.vbuf, b), b == 0, b == KB - 1).then_inc(T.sem["sV%d" % i], 1)
        wdve("sV%d" % i, KB)
        wdve("sR%d" % i, 1)
        dve.tensor_scalar(T["ysb%d" % i][:, :], y, col(i, 2), None, AluOpType.mult).then_inc(T.sem["sY%d" % i], 1)
        r = mine[i]
        if r == core:
            wsp("sY%d" % i, 1)
            sp.dma_start(T.y[:, :], T["ysb%d" % i][:, :]).then_inc(T.sem.done, 16)
            wsp("done", 16)
        else:
            rid, pid, _ = topo.addr(r)
            m = topo.mask(core, r)
            wg("sY%d" % i, 1)
            g.remote_dma(T.yland[:, :], T["ysb%d" % i][:, :], T.sem.yarr, T.sem.sent, pid, rid, m)
            sent[0] += _count(m)

    def pipeline(L):
        m = len(L)
        for j in range(min(NS, m)):
            S(L[j])
        for j in range(m):
            TRPV(L[j])
            if j + NS < m:
                S(L[j + NS])

    if core == owner:
        pipeline([0])
        pipeline(list(range(1, n)))
    else:
        pipeline(list(range(n)))
    if sent[0]:
        g.wait_ge(T.sem.sent, sent[0])


def rank_program(g, core, T, topo):
    owner, work = make_plan(T, topo)
    if core in work:
        worker(g, core, T, topo, owner, work)
    elif T.rank_of(core) is not None:
        client(g, core, T, topo, work)
